import numpy as np
import ml_dtypes


def mxq(x, axis, fmt="e4m3"):
    dtype, down = {"e4m3": (ml_dtypes.float8_e4m3fn, 7), "e5m2": (ml_dtypes.float8_e5m2, 14)}[fmt]
    v = np.moveaxis(np.asarray(x, np.float32).astype(ml_dtypes.bfloat16).astype(np.float64), axis, -1)
    blocks = v.reshape(v.shape[:-1] + (-1, 32))
    amax = np.abs(blocks).max(-1, keepdims=True)
    byte = np.maximum(np.where(amax > 0, np.frexp(amax)[1] - 1 + 127, 0) - down, 1)
    scale = np.exp2(byte - 127.0)
    codes = (blocks / scale).astype(np.float32).astype(dtype).astype(np.float64)
    return np.moveaxis((codes * scale).reshape(v.shape), -1, axis)


WIDE = False


def mx_kscale(k):
    if not WIDE:
        return np.ones(k)
    levels = np.array([10, -10, 5, -5, 0])
    if k % 512:
        return np.exp2(np.random.permutation(np.resize(levels, k // 32))).repeat(32)
    a = np.empty((k // 512, 16))
    for p in range(k // 512):
        a[p, :8] = np.random.permutation(np.resize(levels, 8))
        for g in range(8):
            far = levels[np.abs(levels - a[p, g]) >= 10]
            a[p, g + 8] = far[np.random.randint(len(far))]
    return np.exp2(a.ravel()).repeat(32)


def f64(x):
    return np.asarray(x).astype(np.float64)


def striped(idx):
    return np.tile(idx.reshape(-1, 16).T, (8, 1)).astype(np.uint16)


def unstriped(offs):
    return offs[:16].T.reshape(-1).astype(np.int64)


def silu(v):
    return v / (1.0 + np.exp(-np.maximum(v, -700.0)))


K, T, D, S, V, H, N = 1024, 1024, 2, 512, 256, 1024, 512


def setup_inputs():
    n = np.random.standard_normal
    s = mx_kscale(K)[:, None]
    u = mx_kscale(H)
    return {
        "xT": (n((K, T)) * s).astype(np.float32),
        "w1": (n((K, H)) / np.sqrt(K) / s * u).astype(np.float32),
        "w2": (n((H, N)) / np.sqrt(H) / u[:, None]).astype(np.float32),
        "gate": np.tile(np.random.uniform(0.2, 1.0, (D, 1, V)) / np.sqrt(D), (1, N, 1)).astype(np.float32),
        "offs": striped(np.random.permutation(T)[:S]),
        "pos1": striped(np.random.permutation(S)[:V]),
        "pos2": striped(np.random.permutation(S)[:V]),
    }


def reference(xT, w1, w2, gate, offs, pos1, pos2):
    idx = unstriped(offs)
    xq = mxq(f64(xT)[:, idx], 0, "e4m3")
    h = silu(mxq(f64(w1), 0, "e4m3").T @ xq)
    y = mxq(f64(w2), 0, "e4m3").T @ mxq(h, 0, "e4m3")
    return sum(f64(gate[d]) * y[:, unstriped(p)] for d, p in enumerate((pos1, pos2)))

@@ -1,0 +1,172 @@
+from contextlib import ExitStack
+
+import concourse.mybir as mybir
+
+K, T, S, H, N, V, D = 1024, 1024, 512, 1024, 512, 256, 2
+FLOPS = 2 * S * (K * H + H * N)
+
+F32 = mybir.dt.float32
+BF16 = mybir.dt.bfloat16
+U32 = mybir.dt.uint32
+U16 = mybir.dt.uint16
+U8 = mybir.dt.uint8
+FP8X4 = mybir.dt.float8_e4m3fn_x4
+COPY = mybir.ActivationFunctionType.Copy
+SILU = mybir.ActivationFunctionType.Silu
+MULT = mybir.AluOpType.mult
+ADD = mybir.AluOpType.add
+
+P = 128
+PACK = 4
+PASS = P * PACK
+PASSES = K // PASS
+NB = S // P
+
+X_SCALAR = {(0, 0): 384, (0, 1): 448, (1, 0): 512, (1, 1): 512}
+W1_PIECES = {(0, 0): 1, (0, 1): 1, (1, 0): 1, (1, 1): 2}
+W1_SCALAR = {(0, 0): 80, (0, 1): 48, (1, 0): 24, (1, 1): 20}
+W2_SCALAR = {(0, 0): 0, (0, 1): 32, (1, 0): 0, (1, 1): 8}
+
+
+def tile_picked_sub_mlp_silu_sub_e_kernel(
+    tc, xT, w1, w2, gate, offs, pos1, pos2, out
+):
+    nc = tc.nc
+    with ExitStack() as ctx:
+        keep = ctx.enter_context(tc.tile_pool(name="keep", bufs=1))
+        banks = ctx.enter_context(tc.psum_pool(name="banks", bufs=1))
+
+        def held(shape, dtype, name):
+            return keep.tile(shape, dtype, name=name, align_bytes=64)
+
+        offs_t = keep.tile([P, S // 16], U16, name="offs_t")
+        pos_t = [keep.tile([P, V // 16], U16, name=f"pos_t{d}") for d in range(D)]
+        x_raw = {}
+        for s in range(PASSES):
+            for u in range(2):
+                x_raw[s, u] = held([P, 2, T], F32, f"x_raw{s}{u}")
+                rows = xT[s * PASS : (s + 1) * PASS, :].rearrange("(p j) c -> p j c", j=PACK)
+                nc.sync.dma_start(out=x_raw[s, u][:], in_=rows[:, 2 * u : 2 * u + 2, :])
+                if s == 0 and u == 0:
+                    nc.sync.dma_start(offs_t[:], offs)
+        w1_raw = {}
+        for b in range(H // PASS):
+            for s in range(PASSES):
+                rows = w1[s * PASS : (s + 1) * PASS, :].rearrange("(p j) c -> p j c", j=PACK)
+                width = PASS // W1_PIECES[b, s]
+                w1_raw[b, s] = []
+                for c in range(b * PASS, (b + 1) * PASS, width):
+                    raw = held([P, PACK, width], F32, f"w1_raw{s}_{c}")
+                    nc.sync.dma_start(out=raw[:], in_=rows[:, :, c : c + width])
+                    w1_raw[b, s].append(raw)
+        w2_raw = {}
+        for s in range(PASSES):
+            rows = w2[s * PASS : (s + 1) * PASS, :].rearrange("(p j) c -> p j c", j=PACK)
+            for c in range(2):
+                w2_raw[s, c] = held([P, PACK, N // 2], F32, f"w2_raw{s}{c}")
+                nc.sync.dma_start(out=w2_raw[s, c][:], in_=rows[:, :, c * (N // 2) : (c + 1) * (N // 2)])
+        nc.sync.dma_start(pos_t[0][:], pos1)
+        nc.sync.dma_start(pos_t[1][:], pos2)
+        gates = {}
+        for mt in range(N // P):
+            gates[mt] = held([P, D, V], F32, f"gate{mt}")
+            nc.sync.dma_start(
+                out=gates[mt][:], in_=gate[:, mt * P : (mt + 1) * P, :].rearrange("d p v -> p d v")
+            )
+
+        warm = keep.tile([P, 1], F32, name="warm")
+        nc.vector.memset(warm[:], 0.0)
+        nc.scalar.activation(warm[:], warm[:], SILU)
+
+        def quantise(codes, scales, values):
+            nc.vector.quantize_mx(out=codes.bitcast(FP8X4), scales=scales, in_=values)
+
+        def cast(dst, src, cut):
+            if cut:
+                nc.scalar.activation(dst[:, :cut], src[:, :cut], COPY)
+            nc.vector.tensor_copy(dst[:, cut:], src[:, cut:])
+
+        x_codes, x_scales = {}, {}
+        for s in range(PASSES):
+            picked = held([P, S, PACK], BF16, f"picked{s}")
+            words = picked[:].rearrange("p n j -> p (n j)").bitcast(U32).rearrange("p (n u) -> p n u", u=2)
+            for u in range(2):
+                pairs = held([P, T, 2], BF16, f"pairs{s}{u}")
+                src = x_raw[s, u][:].rearrange("p e c -> p c e")
+                cast(pairs, x_raw[s, u][:].rearrange("p e c -> p c e"), X_SCALAR[s, u])
+                window = pairs[:].rearrange("p c e -> p (c e)").bitcast(U32)
+                nc.vector.tensor_copy(words[:, :, u], window.indirect(offs_t[:]))
+            x_codes[s] = held([P, S], U32, f"x_codes{s}")
+            x_scales[s] = held([P, S], U8, f"x_scales{s}")
+            quantise(x_codes[s][:], x_scales[s][:], picked[:].rearrange("p n j -> p (n j)"))
+
+        w1_codes, w1_scales = {}, {}
+        for b in range(H // PASS):
+            for s in range(PASSES):
+                grouped = held([P, PACK, P, PACK], BF16, f"w1_grouped{b}{s}")
+                dst = grouped[:].rearrange("p t m j -> p m j t")
+                width = P // W1_PIECES[b, s]
+                for c, raw in enumerate(w1_raw[b, s]):
+                    src = raw[:].rearrange("p j (m t) -> p m j t", t=PACK)
+                    cast(dst[:, c * width : (c + 1) * width], src, W1_SCALAR[b, s])
+                w1_codes[b, s] = held([P, PASS], U32, f"w1_codes{b}{s}")
+                w1_scales[b, s] = held([P, PASS], U8, f"w1_scales{b}{s}")
+                quantise(w1_codes[b, s][:], w1_scales[b, s][:], grouped[:].rearrange("p t m j -> p (t m j)"))
+
+        h_codes, h_scales = {}, {}
+        for b in range(H // PASS):
+            h_codes[b] = held([P, S], U32, f"h_codes{b}")
+            h_scales[b] = held([P, S], U8, f"h_scales{b}")
+            for nb in range(NB):
+                cols = slice(nb * P, (nb + 1) * P)
+                acc = banks.tile([P, PACK, P], F32, name=f"acc{nb}")
+                for t in range(PACK):
+                    for s in range(PASSES):
+                        nc.tensor.matmul_mx(
+                            out=acc[:, t, :],
+                            lhsT=w1_codes[b, s][:, t * P : (t + 1) * P].bitcast(FP8X4),
+                            lhsT_scale=w1_scales[b, s][:, t * P : (t + 1) * P],
+                            rhs=x_codes[s][:, cols].bitcast(FP8X4),
+                            rhs_scale=x_scales[s][:, cols],
+                            start=(s == 0),
+                            stop=(s == PASSES - 1),
+                        )
+                h = held([P, P, PACK], BF16, f"h{b}{nb}")
+                nc.scalar.activation(h[:], acc[:].rearrange("p t n -> p n t"), SILU)
+                quantise(h_codes[b][:, cols], h_scales[b][:, cols], h[:].rearrange("p n t -> p (n t)"))
+
+        w2_codes, w2_scales = {}, {}
+        for s in range(PASSES):
+            for c in range(2):
+                grouped = held([P, N // 2, PACK], BF16, f"w2_grouped{s}{c}")
+                dst = grouped[:].rearrange("p (c i) j -> p c j i", i=PACK)
+                src = w2_raw[s, c][:].rearrange("p j (c i) -> p c j i", i=PACK)
+                cast(dst, src, W2_SCALAR[s, c])
+                w2_codes[s, c] = held([P, N // 2], U32, f"w2_codes{s}{c}")
+                w2_scales[s, c] = held([P, N // 2], U8, f"w2_scales{s}{c}")
+                quantise(w2_codes[s, c][:], w2_scales[s, c][:], grouped[:].rearrange("p c j -> p (c j)"))
+        sums = [banks.tile([P, S], F32, name=f"sum{mt}") for mt in range(N // P)]
+        for s in range(PASSES):
+            for mt in range(N // P):
+                cols = slice(mt % 2 * P, (mt % 2 + 1) * P)
+                nc.tensor.matmul_mx(
+                    out=sums[mt][:],
+                    lhsT=w2_codes[s, mt // 2][:, cols].bitcast(FP8X4),
+                    lhsT_scale=w2_scales[s, mt // 2][:, cols],
+                    rhs=h_codes[s][:].bitcast(FP8X4),
+                    rhs_scale=h_scales[s][:],
+                    start=(s == 0),
+                    stop=(s == PASSES - 1),
+                )
+
+        for mt in range(N // P):
+            y = keep.tile([P, S], F32, name=f"y{mt}")
+            nc.scalar.activation(y[:], sums[mt][:], COPY)
+            terms = []
+            for d in range(D):
+                term = keep.tile([P, V], F32, name=f"term{mt}{d}")
+                nc.vector.tensor_tensor(term[:], y[:].indirect(pos_t[d][:]), gates[mt][:, d, :], MULT)
+                terms.append(term)
+            total = keep.tile([P, V], F32, name=f"total{mt}")
+            nc.vector.tensor_tensor(total[:], terms[0][:], terms[1][:], ADD)
+            nc.sync.dma_start(out=out[mt * P : (mt + 1) * P, :], in_=total[:])

@@ -22,10 +22,10 @@ PASS = P * PACK
 PASSES = K // PASS
 NB = S // P
 
-X_SCALAR = {(0, 0): 384, (0, 1): 448, (1, 0): 512, (1, 1): 512}
+X_SCALAR = {(0, 0): 704, (0, 1): 448, (1, 0): 768, (1, 1): 704}
 W1_PIECES = {(0, 0): 1, (0, 1): 1, (1, 0): 1, (1, 1): 2}
-W1_SCALAR = {(0, 0): 80, (0, 1): 48, (1, 0): 24, (1, 1): 20}
-W2_SCALAR = {(0, 0): 0, (0, 1): 32, (1, 0): 0, (1, 1): 8}
+W1_SCALAR = {(0, 0): 120, (0, 1): 72, (1, 0): 40, (1, 1): 16}
+W2_SCALAR = {(0, 0): 8, (0, 1): 0, (1, 0): 0, (1, 1): 64}
 
 
 def tile_picked_sub_mlp_silu_sub_e_kernel(
@@ -60,9 +60,9 @@ def tile_picked_sub_mlp_silu_sub_e_kernel(
                     nc.sync.dma_start(out=raw[:], in_=rows[:, :, c : c + width])
                     w1_raw[b, s].append(raw)
         w2_raw = {}
-        for s in range(PASSES):
-            rows = w2[s * PASS : (s + 1) * PASS, :].rearrange("(p j) c -> p j c", j=PACK)
-            for c in range(2):
+        for c in range(2):
+            for s in range(PASSES):
+                rows = w2[s * PASS : (s + 1) * PASS, :].rearrange("(p j) c -> p j c", j=PACK)
                 w2_raw[s, c] = held([P, PACK, N // 2], F32, f"w2_raw{s}{c}")
                 nc.sync.dma_start(out=w2_raw[s, c][:], in_=rows[:, :, c * (N // 2) : (c + 1) * (N // 2)])
         nc.sync.dma_start(pos_t[0][:], pos1)
@@ -84,7 +84,8 @@ def tile_picked_sub_mlp_silu_sub_e_kernel(
         def cast(dst, src, cut):
             if cut:
                 nc.scalar.activation(dst[:, :cut], src[:, :cut], COPY)
-            nc.vector.tensor_copy(dst[:, cut:], src[:, cut:])
+            if cut < src.shape[1]:
+                nc.vector.tensor_copy(dst[:, cut:], src[:, cut:])
 
         x_codes, x_scales = {}, {}
         for s in range(PASSES):
@@ -120,24 +121,24 @@ def tile_picked_sub_mlp_silu_sub_e_kernel(
             for nb in range(NB):
                 cols = slice(nb * P, (nb + 1) * P)
                 acc = banks.tile([P, PACK, P], F32, name=f"acc{nb}")
-                for t in range(PACK):
-                    for s in range(PASSES):
+                for s in range(PASSES):
+                    for t in range(PACK):
                         nc.tensor.matmul_mx(
                             out=acc[:, t, :],
                             lhsT=w1_codes[b, s][:, t * P : (t + 1) * P].bitcast(FP8X4),
                             lhsT_scale=w1_scales[b, s][:, t * P : (t + 1) * P],
                             rhs=x_codes[s][:, cols].bitcast(FP8X4),
                             rhs_scale=x_scales[s][:, cols],
-                            start=(s == 0),
-                            stop=(s == PASSES - 1),
+                            start=(s == 0 and t == 0),
+                            stop=(s == PASSES - 1 and t == PACK - 1),
                         )
                 h = held([P, P, PACK], BF16, f"h{b}{nb}")
                 nc.scalar.activation(h[:], acc[:].rearrange("p t n -> p n t"), SILU)
                 quantise(h_codes[b][:, cols], h_scales[b][:, cols], h[:].rearrange("p n t -> p (n t)"))
 
         w2_codes, w2_scales = {}, {}
-        for s in range(PASSES):
-            for c in range(2):
+        for c in range(2):
+            for s in range(PASSES):
                 grouped = held([P, N // 2, PACK], BF16, f"w2_grouped{s}{c}")
                 dst = grouped[:].rearrange("p (c i) j -> p c j i", i=PACK)
                 src = w2_raw[s, c][:].rearrange("p j (c i) -> p c j i", i=PACK)
@@ -146,22 +147,33 @@ def tile_picked_sub_mlp_silu_sub_e_kernel(
                 w2_scales[s, c] = held([P, N // 2], U8, f"w2_scales{s}{c}")
                 quantise(w2_codes[s, c][:], w2_scales[s, c][:], grouped[:].rearrange("p c j -> p (c j)"))
         sums = [banks.tile([P, S], F32, name=f"sum{mt}") for mt in range(N // P)]
+
+        def product2(mt, s, cols):
+            w_cols = slice(mt % 2 * P, (mt % 2 + 1) * P)
+            nc.tensor.matmul_mx(
+                out=sums[mt][:, cols],
+                lhsT=w2_codes[s, mt // 2][:, w_cols].bitcast(FP8X4),
+                lhsT_scale=w2_scales[s, mt // 2][:, w_cols],
+                rhs=h_codes[s][:, cols].bitcast(FP8X4),
+                rhs_scale=h_scales[s][:, cols],
+                start=(s == 0),
+                stop=(s == PASSES - 1),
+            )
+
+        for nb in range(NB):
+            for s in range(PASSES):
+                product2(0, s, slice(nb * P, (nb + 1) * P))
         for s in range(PASSES):
-            for mt in range(N // P):
-                cols = slice(mt % 2 * P, (mt % 2 + 1) * P)
-                nc.tensor.matmul_mx(
-                    out=sums[mt][:],
-                    lhsT=w2_codes[s, mt // 2][:, cols].bitcast(FP8X4),
-                    lhsT_scale=w2_scales[s, mt // 2][:, cols],
-                    rhs=h_codes[s][:].bitcast(FP8X4),
-                    rhs_scale=h_scales[s][:],
-                    start=(s == 0),
-                    stop=(s == PASSES - 1),
-                )
+            for mt in range(1, N // P):
+                product2(mt, s, slice(0, S))
 
         for mt in range(N // P):
             y = keep.tile([P, S], F32, name=f"y{mt}")
-            nc.scalar.activation(y[:], sums[mt][:], COPY)
+            if mt == 0:
+                nc.scalar.activation(y[:, : S - P], sums[mt][:, : S - P], COPY)
+                nc.vector.tensor_copy(y[:, S - P :], sums[mt][:, S - P :])
+            else:
+                nc.scalar.activation(y[:], sums[mt][:], COPY)
             terms = []
             for d in range(D):
                 term = keep.tile([P, V], F32, name=f"term{mt}{d}")

@@ -22,10 +22,9 @@ PASS = P * PACK
 PASSES = K // PASS
 NB = S // P
 
-X_SCALAR = {(0, 0): 704, (0, 1): 448, (1, 0): 768, (1, 1): 704}
-W1_PIECES = {(0, 0): 1, (0, 1): 1, (1, 0): 1, (1, 1): 2}
-W1_SCALAR = {(0, 0): 120, (0, 1): 72, (1, 0): 40, (1, 1): 16}
-W2_SCALAR = {(0, 0): 8, (0, 1): 0, (1, 0): 0, (1, 1): 64}
+X_SCALAR = {(0, 0): 256, (0, 1): 448, (1, 0): 768, (1, 1): 704}
+W1_SCALAR = {(0, 0): 80, (0, 1): 56, (1, 0): 48, (1, 1): 32}
+W2_SCALAR = {(0, 0): 0, (0, 1): 8, (1, 0): 0, (1, 1): 40}
 
 
 def tile_picked_sub_mlp_silu_sub_e_kernel(
@@ -50,21 +49,22 @@ def tile_picked_sub_mlp_silu_sub_e_kernel(
                 if s == 0 and u == 0:
                     nc.sync.dma_start(offs_t[:], offs)
         w1_raw = {}
+        rows = w1[:PASS, :].rearrange("(p j) c -> p j c", j=PACK)
+        raw = held([P, PACK, H], F32, "w1_raw0")
+        nc.sync.dma_start(out=raw[:], in_=rows)
         for b in range(H // PASS):
-            for s in range(PASSES):
-                rows = w1[s * PASS : (s + 1) * PASS, :].rearrange("(p j) c -> p j c", j=PACK)
-                width = PASS // W1_PIECES[b, s]
-                w1_raw[b, s] = []
-                for c in range(b * PASS, (b + 1) * PASS, width):
-                    raw = held([P, PACK, width], F32, f"w1_raw{s}_{c}")
-                    nc.sync.dma_start(out=raw[:], in_=rows[:, :, c : c + width])
-                    w1_raw[b, s].append(raw)
+            w1_raw[b, 0] = raw[:, :, b * PASS : (b + 1) * PASS]
+        rows = w1[PASS:, :].rearrange("(p j) c -> p j c", j=PACK)
+        for b in range(H // PASS):
+            raw = held([P, PACK, PASS], F32, f"w1_raw1{b}")
+            nc.sync.dma_start(out=raw[:], in_=rows[:, :, b * PASS : (b + 1) * PASS])
+            w1_raw[b, 1] = raw[:]
         w2_raw = {}
-        for c in range(2):
-            for s in range(PASSES):
-                rows = w2[s * PASS : (s + 1) * PASS, :].rearrange("(p j) c -> p j c", j=PACK)
-                w2_raw[s, c] = held([P, PACK, N // 2], F32, f"w2_raw{s}{c}")
-                nc.sync.dma_start(out=w2_raw[s, c][:], in_=rows[:, :, c * (N // 2) : (c + 1) * (N // 2)])
+        for s in range(PASSES):
+            w2_raw[s] = held([P, PACK, N], F32, f"w2_raw{s}")
+            nc.sync.dma_start(
+                out=w2_raw[s][:], in_=w2[s * PASS : (s + 1) * PASS, :].rearrange("(p j) c -> p j c", j=PACK)
+            )
         nc.sync.dma_start(pos_t[0][:], pos1)
         nc.sync.dma_start(pos_t[1][:], pos2)
         gates = {}
@@ -106,10 +106,7 @@ def tile_picked_sub_mlp_silu_sub_e_kernel(
             for s in range(PASSES):
                 grouped = held([P, PACK, P, PACK], BF16, f"w1_grouped{b}{s}")
                 dst = grouped[:].rearrange("p t m j -> p m j t")
-                width = P // W1_PIECES[b, s]
-                for c, raw in enumerate(w1_raw[b, s]):
-                    src = raw[:].rearrange("p j (m t) -> p m j t", t=PACK)
-                    cast(dst[:, c * width : (c + 1) * width], src, W1_SCALAR[b, s])
+                cast(dst, w1_raw[b, s].rearrange("p j (m t) -> p m j t", t=PACK), W1_SCALAR[b, s])
                 w1_codes[b, s] = held([P, PASS], U32, f"w1_codes{b}{s}")
                 w1_scales[b, s] = held([P, PASS], U8, f"w1_scales{b}{s}")
                 quantise(w1_codes[b, s][:], w1_scales[b, s][:], grouped[:].rearrange("p t m j -> p (t m j)"))
@@ -141,7 +138,7 @@ def tile_picked_sub_mlp_silu_sub_e_kernel(
             for s in range(PASSES):
                 grouped = held([P, N // 2, PACK], BF16, f"w2_grouped{s}{c}")
                 dst = grouped[:].rearrange("p (c i) j -> p c j i", i=PACK)
-                src = w2_raw[s, c][:].rearrange("p j (c i) -> p c j i", i=PACK)
+                src = w2_raw[s][:, :, c * (N // 2) : (c + 1) * (N // 2)].rearrange("p j (c i) -> p c j i", i=PACK)
                 cast(dst, src, W2_SCALAR[s, c])
                 w2_codes[s, c] = held([P, N // 2], U32, f"w2_codes{s}{c}")
                 w2_scales[s, c] = held([P, N // 2], U8, f"w2_scales{s}{c}")
@@ -167,18 +164,20 @@ def tile_picked_sub_mlp_silu_sub_e_kernel(
             for mt in range(1, N // P):
                 product2(mt, s, slice(0, S))
 
+        terms = {}
+
+        def finish(mt):
+            total = keep.tile([P, V], F32, name=f"total{mt}")
+            nc.vector.tensor_tensor(total[:], terms[mt, 0][:], terms[mt, 1][:], ADD)
+            nc.sync.dma_start(out=out[mt * P : (mt + 1) * P, :], in_=total[:])
+
         for mt in range(N // P):
             y = keep.tile([P, S], F32, name=f"y{mt}")
-            if mt == 0:
-                nc.scalar.activation(y[:, : S - P], sums[mt][:, : S - P], COPY)
-                nc.vector.tensor_copy(y[:, S - P :], sums[mt][:, S - P :])
-            else:
-                nc.scalar.activation(y[:], sums[mt][:], COPY)
-            terms = []
+            for cols in (slice(0, S - P), slice(S - P, S)) if mt == 0 else (slice(0, S),):
+                nc.scalar.activation(y[:, cols], sums[mt][:, cols], COPY)
             for d in range(D):
-                term = keep.tile([P, V], F32, name=f"term{mt}{d}")
-                nc.vector.tensor_tensor(term[:], y[:].indirect(pos_t[d][:]), gates[mt][:, d, :], MULT)
-                terms.append(term)
-            total = keep.tile([P, V], F32, name=f"total{mt}")
-            nc.vector.tensor_tensor(total[:], terms[0][:], terms[1][:], ADD)
-            nc.sync.dma_start(out=out[mt * P : (mt + 1) * P, :], in_=total[:])
+                terms[mt, d] = keep.tile([P, V], F32, name=f"term{mt}{d}")
+                nc.vector.tensor_tensor(terms[mt, d][:], y[:].indirect(pos_t[d][:]), gates[mt][:, d, :], MULT)
+                if mt > 0 and d == 0:
+                    finish(mt - 1)
+        finish(N // P - 1)

@@ -22,9 +22,9 @@ PASS = P * PACK
 PASSES = K // PASS
 NB = S // P
 
-X_SCALAR = {(0, 0): 256, (0, 1): 448, (1, 0): 768, (1, 1): 704}
-W1_SCALAR = {(0, 0): 80, (0, 1): 56, (1, 0): 48, (1, 1): 32}
-W2_SCALAR = {(0, 0): 0, (0, 1): 8, (1, 0): 0, (1, 1): 40}
+X_SCALAR = {(0, 0): 384, (0, 1): 512, (1, 0): 768, (1, 1): 704}
+W1_SCALAR = {(0, 0): (80,), (0, 1): (40,), (1, 0): (48,), (1, 1): (16, 4)}
+W2_SCALAR = {(0, 0): 0, (0, 1): 24, (1, 0): 0, (1, 1): 64}
 
 
 def tile_picked_sub_mlp_silu_sub_e_kernel(
@@ -53,12 +53,14 @@ def tile_picked_sub_mlp_silu_sub_e_kernel(
         raw = held([P, PACK, H], F32, "w1_raw0")
         nc.sync.dma_start(out=raw[:], in_=rows)
         for b in range(H // PASS):
-            w1_raw[b, 0] = raw[:, :, b * PASS : (b + 1) * PASS]
+            w1_raw[b, 0] = [raw[:, :, b * PASS : (b + 1) * PASS]]
         rows = w1[PASS:, :].rearrange("(p j) c -> p j c", j=PACK)
-        for b in range(H // PASS):
-            raw = held([P, PACK, PASS], F32, f"w1_raw1{b}")
-            nc.sync.dma_start(out=raw[:], in_=rows[:, :, b * PASS : (b + 1) * PASS])
-            w1_raw[b, 1] = raw[:]
+        for b, width in ((0, PASS), (1, PASS // 2)):
+            w1_raw[b, 1] = []
+            for c in range(b * PASS, (b + 1) * PASS, width):
+                raw = held([P, PACK, width], F32, f"w1_raw1{c}")
+                nc.sync.dma_start(out=raw[:], in_=rows[:, :, c : c + width])
+                w1_raw[b, 1].append(raw[:])
         w2_raw = {}
         for s in range(PASSES):
             w2_raw[s] = held([P, PACK, N], F32, f"w2_raw{s}")
@@ -102,17 +104,21 @@ def tile_picked_sub_mlp_silu_sub_e_kernel(
             quantise(x_codes[s][:], x_scales[s][:], picked[:].rearrange("p n j -> p (n j)"))
 
         w1_codes, w1_scales = {}, {}
-        for b in range(H // PASS):
-            for s in range(PASSES):
-                grouped = held([P, PACK, P, PACK], BF16, f"w1_grouped{b}{s}")
-                dst = grouped[:].rearrange("p t m j -> p m j t")
-                cast(dst, w1_raw[b, s].rearrange("p j (m t) -> p m j t", t=PACK), W1_SCALAR[b, s])
-                w1_codes[b, s] = held([P, PASS], U32, f"w1_codes{b}{s}")
-                w1_scales[b, s] = held([P, PASS], U8, f"w1_scales{b}{s}")
-                quantise(w1_codes[b, s][:], w1_scales[b, s][:], grouped[:].rearrange("p t m j -> p (t m j)"))
+
+        def prepare_w1(b, s):
+            grouped = held([P, PACK, P, PACK], BF16, f"w1_grouped{b}{s}")
+            dst = grouped[:].rearrange("p t m j -> p m j t")
+            width = P // len(w1_raw[b, s])
+            for c, raw in enumerate(w1_raw[b, s]):
+                src = raw.rearrange("p j (m t) -> p m j t", t=PACK)
+                cast(dst[:, c * width : (c + 1) * width], src, W1_SCALAR[b, s][c])
+            w1_codes[b, s] = held([P, PASS], U32, f"w1_codes{b}{s}")
+            w1_scales[b, s] = held([P, PASS], U8, f"w1_scales{b}{s}")
+            quantise(w1_codes[b, s][:], w1_scales[b, s][:], grouped[:].rearrange("p t m j -> p (t m j)"))
 
         h_codes, h_scales = {}, {}
-        for b in range(H // PASS):
+
+        def product1(b):
             h_codes[b] = held([P, S], U32, f"h_codes{b}")
             h_scales[b] = held([P, S], U8, f"h_scales{b}")
             for nb in range(NB):
@@ -133,36 +139,42 @@ def tile_picked_sub_mlp_silu_sub_e_kernel(
                 nc.scalar.activation(h[:], acc[:].rearrange("p t n -> p n t"), SILU)
                 quantise(h_codes[b][:, cols], h_scales[b][:, cols], h[:].rearrange("p n t -> p (n t)"))
 
-        w2_codes, w2_scales = {}, {}
+        prepare_w1(0, 0)
+        prepare_w1(0, 1)
+        prepare_w1(1, 0)
+        product1(0)
+        prepare_w1(1, 1)
+        product1(1)
+
+        y = {}
         for c in range(2):
+            w2_codes, w2_scales = {}, {}
             for s in range(PASSES):
                 grouped = held([P, N // 2, PACK], BF16, f"w2_grouped{s}{c}")
                 dst = grouped[:].rearrange("p (c i) j -> p c j i", i=PACK)
                 src = w2_raw[s][:, :, c * (N // 2) : (c + 1) * (N // 2)].rearrange("p j (c i) -> p c j i", i=PACK)
                 cast(dst, src, W2_SCALAR[s, c])
-                w2_codes[s, c] = held([P, N // 2], U32, f"w2_codes{s}{c}")
-                w2_scales[s, c] = held([P, N // 2], U8, f"w2_scales{s}{c}")
-                quantise(w2_codes[s, c][:], w2_scales[s, c][:], grouped[:].rearrange("p c j -> p (c j)"))
-        sums = [banks.tile([P, S], F32, name=f"sum{mt}") for mt in range(N // P)]
-
-        def product2(mt, s, cols):
-            w_cols = slice(mt % 2 * P, (mt % 2 + 1) * P)
-            nc.tensor.matmul_mx(
-                out=sums[mt][:, cols],
-                lhsT=w2_codes[s, mt // 2][:, w_cols].bitcast(FP8X4),
-                lhsT_scale=w2_scales[s, mt // 2][:, w_cols],
-                rhs=h_codes[s][:, cols].bitcast(FP8X4),
-                rhs_scale=h_scales[s][:, cols],
-                start=(s == 0),
-                stop=(s == PASSES - 1),
-            )
-
-        for nb in range(NB):
-            for s in range(PASSES):
-                product2(0, s, slice(nb * P, (nb + 1) * P))
-        for s in range(PASSES):
-            for mt in range(1, N // P):
-                product2(mt, s, slice(0, S))
+                w2_codes[s] = held([P, N // 2], U32, f"w2_codes{s}{c}")
+                w2_scales[s] = held([P, N // 2], U8, f"w2_scales{s}{c}")
+                quantise(w2_codes[s][:], w2_scales[s][:], grouped[:].rearrange("p c j -> p (c j)"))
+            for mt in (2 * c, 2 * c + 1):
+                total = banks.tile([P, S], F32, name=f"sum{mt}")
+                y[mt] = keep.tile([P, S], F32, name=f"y{mt}")
+                pieces = [slice(nb * P, (nb + 1) * P) for nb in range(NB)] if mt == 0 else [slice(0, S)]
+                for cols in pieces:
+                    for s in range(PASSES):
+                        w_cols = slice(mt % 2 * P, (mt % 2 + 1) * P)
+                        nc.tensor.matmul_mx(
+                            out=total[:, cols],
+                            lhsT=w2_codes[s][:, w_cols].bitcast(FP8X4),
+                            lhsT_scale=w2_scales[s][:, w_cols],
+                            rhs=h_codes[s][:, cols].bitcast(FP8X4),
+                            rhs_scale=h_scales[s][:, cols],
+                            start=(s == 0),
+                            stop=(s == PASSES - 1),
+                        )
+                for cols in (slice(0, S - P), slice(S - P, S)) if mt == 0 else (slice(0, S),):
+                    nc.scalar.activation(y[mt][:, cols], total[:, cols], COPY)
 
         terms = {}
 
@@ -172,12 +184,9 @@ def tile_picked_sub_mlp_silu_sub_e_kernel(
             nc.sync.dma_start(out=out[mt * P : (mt + 1) * P, :], in_=total[:])
 
         for mt in range(N // P):
-            y = keep.tile([P, S], F32, name=f"y{mt}")
-            for cols in (slice(0, S - P), slice(S - P, S)) if mt == 0 else (slice(0, S),):
-                nc.scalar.activation(y[:, cols], sums[mt][:, cols], COPY)
             for d in range(D):
                 terms[mt, d] = keep.tile([P, V], F32, name=f"term{mt}{d}")
-                nc.vector.tensor_tensor(terms[mt, d][:], y[:].indirect(pos_t[d][:]), gates[mt][:, d, :], MULT)
+                nc.vector.tensor_tensor(terms[mt, d][:], y[mt][:].indirect(pos_t[d][:]), gates[mt][:, d, :], MULT)
                 if mt > 0 and d == 0:
                     finish(mt - 1)
         finish(N // P - 1)

@@ -24,6 +24,7 @@ NB = S // P
 
 X_SCALAR = {(0, 0): 384, (0, 1): 512, (1, 0): 768, (1, 1): 704}
 W1_SCALAR = {(0, 0): (80,), (0, 1): (40,), (1, 0): (48,), (1, 1): (16, 4)}
+H_BLOCKS = (4, 1)
 W2_SCALAR = {(0, 0): 0, (0, 1): 24, (1, 0): 0, (1, 1): 64}
 
 
@@ -119,6 +120,7 @@ def tile_picked_sub_mlp_silu_sub_e_kernel(
         h_codes, h_scales = {}, {}
 
         def product1(b):
+            h = held([P, S, PACK], BF16, f"h{b}")
             h_codes[b] = held([P, S], U32, f"h_codes{b}")
             h_scales[b] = held([P, S], U8, f"h_scales{b}")
             for nb in range(NB):
@@ -135,9 +137,10 @@ def tile_picked_sub_mlp_silu_sub_e_kernel(
                             start=(s == 0 and t == 0),
                             stop=(s == PASSES - 1 and t == PACK - 1),
                         )
-                h = held([P, P, PACK], BF16, f"h{b}{nb}")
-                nc.scalar.activation(h[:], acc[:].rearrange("p t n -> p n t"), SILU)
-                quantise(h_codes[b][:, cols], h_scales[b][:, cols], h[:].rearrange("p n t -> p (n t)"))
+                nc.scalar.activation(h[:, cols, :], acc[:].rearrange("p t n -> p n t"), SILU)
+                if (nb + 1) % H_BLOCKS[b] == 0:
+                    ready = slice((nb + 1 - H_BLOCKS[b]) * P, (nb + 1) * P)
+                    quantise(h_codes[b][:, ready], h_scales[b][:, ready], h[:, ready, :].rearrange("p n t -> p (n t)"))
 
         prepare_w1(0, 0)
         prepare_w1(0, 1)
@@ -148,15 +151,21 @@ def tile_picked_sub_mlp_silu_sub_e_kernel(
 
         y = {}
         for c in range(2):
-            w2_codes, w2_scales = {}, {}
+            grouped = held([P, PASSES, N // 2, PACK], BF16, f"w2_grouped{c}")
+            w2_codes = held([P, PASSES, N // 2], U32, f"w2_codes{c}")
+            w2_scales = held([P, PASSES, N // 2], U8, f"w2_scales{c}")
             for s in range(PASSES):
-                grouped = held([P, N // 2, PACK], BF16, f"w2_grouped{s}{c}")
-                dst = grouped[:].rearrange("p (c i) j -> p c j i", i=PACK)
+                dst = grouped[:, s].rearrange("p (c i) j -> p c j i", i=PACK)
                 src = w2_raw[s][:, :, c * (N // 2) : (c + 1) * (N // 2)].rearrange("p j (c i) -> p c j i", i=PACK)
                 cast(dst, src, W2_SCALAR[s, c])
-                w2_codes[s] = held([P, N // 2], U32, f"w2_codes{s}{c}")
-                w2_scales[s] = held([P, N // 2], U8, f"w2_scales{s}{c}")
-                quantise(w2_codes[s][:], w2_scales[s][:], grouped[:].rearrange("p c j -> p (c j)"))
+                if c == 0:
+                    quantise(w2_codes[:, s], w2_scales[:, s], grouped[:, s].rearrange("p c j -> p (c j)"))
+            if c == 1:
+                quantise(
+                    w2_codes[:].rearrange("p s c -> p (s c)"),
+                    w2_scales[:].rearrange("p s c -> p (s c)"),
+                    grouped[:].rearrange("p s c j -> p (s c j)"),
+                )
             for mt in (2 * c, 2 * c + 1):
                 total = banks.tile([P, S], F32, name=f"sum{mt}")
                 y[mt] = keep.tile([P, S], F32, name=f"y{mt}")
@@ -166,8 +175,8 @@ def tile_picked_sub_mlp_silu_sub_e_kernel(
                         w_cols = slice(mt % 2 * P, (mt % 2 + 1) * P)
                         nc.tensor.matmul_mx(
                             out=total[:, cols],
-                            lhsT=w2_codes[s][:, w_cols].bitcast(FP8X4),
-                            lhsT_scale=w2_scales[s][:, w_cols],
+                            lhsT=w2_codes[:, s, w_cols].bitcast(FP8X4),
+                            lhsT_scale=w2_scales[:, s, w_cols],
                             rhs=h_codes[s][:, cols].bitcast(FP8X4),
                             rhs_scale=h_scales[s][:, cols],
                             start=(s == 0),
@@ -176,17 +185,23 @@ def tile_picked_sub_mlp_silu_sub_e_kernel(
                 for cols in (slice(0, S - P), slice(S - P, S)) if mt == 0 else (slice(0, S),):
                     nc.scalar.activation(y[mt][:, cols], total[:, cols], COPY)
 
-        terms = {}
+        out_rows = out.rearrange("(m p) v -> p m v", p=P)
 
-        def finish(mt):
-            total = keep.tile([P, V], F32, name=f"total{mt}")
-            nc.vector.tensor_tensor(total[:], terms[mt, 0][:], terms[mt, 1][:], ADD)
-            nc.sync.dma_start(out=out[mt * P : (mt + 1) * P, :], in_=total[:])
+        def finish(mts, terms):
+            total = keep.tile([P, len(mts), V], F32, name=f"total{mts[0]}")
+            nc.vector.tensor_tensor(total[:], terms[0][:], terms[1][:], ADD)
+            nc.sync.dma_start(out=out_rows[:, mts[0] : mts[-1] + 1, :], in_=total[:])
 
-        for mt in range(N // P):
-            for d in range(D):
-                terms[mt, d] = keep.tile([P, V], F32, name=f"term{mt}{d}")
-                nc.vector.tensor_tensor(terms[mt, d][:], y[mt][:].indirect(pos_t[d][:]), gates[mt][:, d, :], MULT)
-                if mt > 0 and d == 0:
-                    finish(mt - 1)
-        finish(N // P - 1)
+        waiting = None
+        for mts in ((0, 1), (2,), (3,)):
+            terms = [keep.tile([P, len(mts), V], F32, name=f"term{mts[0]}{d}") for d in range(D)]
+            for i, mt in enumerate(mts):
+                for d in range(D):
+                    nc.vector.tensor_tensor(
+                        terms[d][:, i, :], y[mt][:].indirect(pos_t[d][:]), gates[mt][:, d, :], MULT
+                    )
+                    if waiting:
+                        finish(*waiting)
+                        waiting = None
+            waiting = (mts, terms)
+        finish(*waiting)

from contextlib import ExitStack

import concourse.mybir as mybir

K, T, S, H, N, V, D = 1024, 1024, 512, 1024, 512, 256, 2
FLOPS = 2 * S * (K * H + H * N)

F32 = mybir.dt.float32
BF16 = mybir.dt.bfloat16
U32 = mybir.dt.uint32
U16 = mybir.dt.uint16
U8 = mybir.dt.uint8
FP8X4 = mybir.dt.float8_e4m3fn_x4
COPY = mybir.ActivationFunctionType.Copy
SILU = mybir.ActivationFunctionType.Silu
MULT = mybir.AluOpType.mult
ADD = mybir.AluOpType.add

P = 128
PACK = 4
PASS = P * PACK
PASSES = K // PASS
NB = S // P

X_SCALAR = {(0, 0): 384, (0, 1): 512, (1, 0): 768, (1, 1): 704}
W1_SCALAR = {(0, 0): (80,), (0, 1): (40,), (1, 0): (48,), (1, 1): (16, 4)}
H_BLOCKS = (4, 1)
W2_SCALAR = {(0, 0): 0, (0, 1): 24, (1, 0): 0, (1, 1): 64}


def tile_picked_sub_mlp_silu_sub_e_kernel(
    tc, xT, w1, w2, gate, offs, pos1, pos2, out
):
    nc = tc.nc
    with ExitStack() as ctx:
        keep = ctx.enter_context(tc.tile_pool(name="keep", bufs=1))
        banks = ctx.enter_context(tc.psum_pool(name="banks", bufs=1))

        def held(shape, dtype, name):
            return keep.tile(shape, dtype, name=name, align_bytes=64)

        offs_t = keep.tile([P, S // 16], U16, name="offs_t")
        pos_t = [keep.tile([P, V // 16], U16, name=f"pos_t{d}") for d in range(D)]
        x_raw = {}
        for s in range(PASSES):
            for u in range(2):
                x_raw[s, u] = held([P, 2, T], F32, f"x_raw{s}{u}")
                rows = xT[s * PASS : (s + 1) * PASS, :].rearrange("(p j) c -> p j c", j=PACK)
                nc.sync.dma_start(out=x_raw[s, u][:], in_=rows[:, 2 * u : 2 * u + 2, :])
                if s == 0 and u == 0:
                    nc.sync.dma_start(offs_t[:], offs)
        w1_raw = {}
        rows = w1[:PASS, :].rearrange("(p j) c -> p j c", j=PACK)
        raw = held([P, PACK, H], F32, "w1_raw0")
        nc.sync.dma_start(out=raw[:], in_=rows)
        for b in range(H // PASS):
            w1_raw[b, 0] = [raw[:, :, b * PASS : (b + 1) * PASS]]
        rows = w1[PASS:, :].rearrange("(p j) c -> p j c", j=PACK)
        for b, width in ((0, PASS), (1, PASS // 2)):
            w1_raw[b, 1] = []
            for c in range(b * PASS, (b + 1) * PASS, width):
                raw = held([P, PACK, width], F32, f"w1_raw1{c}")
                nc.sync.dma_start(out=raw[:], in_=rows[:, :, c : c + width])
                w1_raw[b, 1].append(raw[:])
        w2_raw = {}
        for s in range(PASSES):
            w2_raw[s] = held([P, PACK, N], F32, f"w2_raw{s}")
            nc.sync.dma_start(
                out=w2_raw[s][:], in_=w2[s * PASS : (s + 1) * PASS, :].rearrange("(p j) c -> p j c", j=PACK)
            )
        nc.sync.dma_start(pos_t[0][:], pos1)
        nc.sync.dma_start(pos_t[1][:], pos2)
        gates = {}
        for mt in range(N // P):
            gates[mt] = held([P, D, V], F32, f"gate{mt}")
            nc.sync.dma_start(
                out=gates[mt][:], in_=gate[:, mt * P : (mt + 1) * P, :].rearrange("d p v -> p d v")
            )

        warm = keep.tile([P, 1], F32, name="warm")
        nc.vector.memset(warm[:], 0.0)
        nc.scalar.activation(warm[:], warm[:], SILU)

        def quantise(codes, scales, values):
            nc.vector.quantize_mx(out=codes.bitcast(FP8X4), scales=scales, in_=values)

        def cast(dst, src, cut):
            if cut:
                nc.scalar.activation(dst[:, :cut], src[:, :cut], COPY)
            if cut < src.shape[1]:
                nc.vector.tensor_copy(dst[:, cut:], src[:, cut:])

        x_codes, x_scales = {}, {}
        for s in range(PASSES):
            picked = held([P, S, PACK], BF16, f"picked{s}")
            words = picked[:].rearrange("p n j -> p (n j)").bitcast(U32).rearrange("p (n u) -> p n u", u=2)
            for u in range(2):
                pairs = held([P, T, 2], BF16, f"pairs{s}{u}")
                src = x_raw[s, u][:].rearrange("p e c -> p c e")
                cast(pairs, x_raw[s, u][:].rearrange("p e c -> p c e"), X_SCALAR[s, u])
                window = pairs[:].rearrange("p c e -> p (c e)").bitcast(U32)
                nc.vector.tensor_copy(words[:, :, u], window.indirect(offs_t[:]))
            x_codes[s] = held([P, S], U32, f"x_codes{s}")
            x_scales[s] = held([P, S], U8, f"x_scales{s}")
            quantise(x_codes[s][:], x_scales[s][:], picked[:].rearrange("p n j -> p (n j)"))

        w1_codes, w1_scales = {}, {}

        def prepare_w1(b, s):
            grouped = held([P, PACK, P, PACK], BF16, f"w1_grouped{b}{s}")
            dst = grouped[:].rearrange("p t m j -> p m j t")
            width = P // len(w1_raw[b, s])
            for c, raw in enumerate(w1_raw[b, s]):
                src = raw.rearrange("p j (m t) -> p m j t", t=PACK)
                cast(dst[:, c * width : (c + 1) * width], src, W1_SCALAR[b, s][c])
            w1_codes[b, s] = held([P, PASS], U32, f"w1_codes{b}{s}")
            w1_scales[b, s] = held([P, PASS], U8, f"w1_scales{b}{s}")
            quantise(w1_codes[b, s][:], w1_scales[b, s][:], grouped[:].rearrange("p t m j -> p (t m j)"))

        h_codes, h_scales = {}, {}

        def product1(b):
            h = held([P, S, PACK], BF16, f"h{b}")
            h_codes[b] = held([P, S], U32, f"h_codes{b}")
            h_scales[b] = held([P, S], U8, f"h_scales{b}")
            for nb in range(NB):
                cols = slice(nb * P, (nb + 1) * P)
                acc = banks.tile([P, PACK, P], F32, name=f"acc{nb}")
                for s in range(PASSES):
                    for t in range(PACK):
                        nc.tensor.matmul_mx(
                            out=acc[:, t, :],
                            lhsT=w1_codes[b, s][:, t * P : (t + 1) * P].bitcast(FP8X4),
                            lhsT_scale=w1_scales[b, s][:, t * P : (t + 1) * P],
                            rhs=x_codes[s][:, cols].bitcast(FP8X4),
                            rhs_scale=x_scales[s][:, cols],
                            start=(s == 0 and t == 0),
                            stop=(s == PASSES - 1 and t == PACK - 1),
                        )
                nc.scalar.activation(h[:, cols, :], acc[:].rearrange("p t n -> p n t"), SILU)
                if (nb + 1) % H_BLOCKS[b] == 0:
                    ready = slice((nb + 1 - H_BLOCKS[b]) * P, (nb + 1) * P)
                    quantise(h_codes[b][:, ready], h_scales[b][:, ready], h[:, ready, :].rearrange("p n t -> p (n t)"))

        prepare_w1(0, 0)
        prepare_w1(0, 1)
        prepare_w1(1, 0)
        product1(0)
        prepare_w1(1, 1)
        product1(1)

        y = {}
        for c in range(2):
            grouped = held([P, PASSES, N // 2, PACK], BF16, f"w2_grouped{c}")
            w2_codes = held([P, PASSES, N // 2], U32, f"w2_codes{c}")
            w2_scales = held([P, PASSES, N // 2], U8, f"w2_scales{c}")
            for s in range(PASSES):
                dst = grouped[:, s].rearrange("p (c i) j -> p c j i", i=PACK)
                src = w2_raw[s][:, :, c * (N // 2) : (c + 1) * (N // 2)].rearrange("p j (c i) -> p c j i", i=PACK)
                cast(dst, src, W2_SCALAR[s, c])
                if c == 0:
                    quantise(w2_codes[:, s], w2_scales[:, s], grouped[:, s].rearrange("p c j -> p (c j)"))
            if c == 1:
                quantise(
                    w2_codes[:].rearrange("p s c -> p (s c)"),
                    w2_scales[:].rearrange("p s c -> p (s c)"),
                    grouped[:].rearrange("p s c j -> p (s c j)"),
                )
            for mt in (2 * c, 2 * c + 1):
                total = banks.tile([P, S], F32, name=f"sum{mt}")
                y[mt] = keep.tile([P, S], F32, name=f"y{mt}")
                pieces = [slice(nb * P, (nb + 1) * P) for nb in range(NB)] if mt == 0 else [slice(0, S)]
                for cols in pieces:
                    for s in range(PASSES):
                        w_cols = slice(mt % 2 * P, (mt % 2 + 1) * P)
                        nc.tensor.matmul_mx(
                            out=total[:, cols],
                            lhsT=w2_codes[:, s, w_cols].bitcast(FP8X4),
                            lhsT_scale=w2_scales[:, s, w_cols],
                            rhs=h_codes[s][:, cols].bitcast(FP8X4),
                            rhs_scale=h_scales[s][:, cols],
                            start=(s == 0),
                            stop=(s == PASSES - 1),
                        )
                for cols in (slice(0, S - P), slice(S - P, S)) if mt == 0 else (slice(0, S),):
                    nc.scalar.activation(y[mt][:, cols], total[:, cols], COPY)

        out_rows = out.rearrange("(m p) v -> p m v", p=P)

        def finish(mts, terms):
            total = keep.tile([P, len(mts), V], F32, name=f"total{mts[0]}")
            nc.vector.tensor_tensor(total[:], terms[0][:], terms[1][:], ADD)
            nc.sync.dma_start(out=out_rows[:, mts[0] : mts[-1] + 1, :], in_=total[:])

        waiting = None
        for mts in ((0, 1), (2,), (3,)):
            terms = [keep.tile([P, len(mts), V], F32, name=f"term{mts[0]}{d}") for d in range(D)]
            for i, mt in enumerate(mts):
                for d in range(D):
                    nc.vector.tensor_tensor(
                        terms[d][:, i, :], y[mt][:].indirect(pos_t[d][:]), gates[mt][:, d, :], MULT
                    )
                    if waiting:
                        finish(*waiting)
                        waiting = None
            waiting = (mts, terms)
        finish(*waiting)
